import numpy as np
import ml_dtypes


def mxq(x, axis, fmt="e4m3"):
    dtype, down = {"e4m3": (ml_dtypes.float8_e4m3fn, 7), "e5m2": (ml_dtypes.float8_e5m2, 14)}[fmt]
    v = np.moveaxis(np.asarray(x, np.float32).astype(ml_dtypes.bfloat16).astype(np.float64), axis, -1)
    blocks = v.reshape(v.shape[:-1] + (-1, 32))
    amax = np.abs(blocks).max(-1, keepdims=True)
    byte = np.maximum(np.where(amax > 0, np.frexp(amax)[1] - 1 + 127, 0) - down, 1)
    scale = np.exp2(byte - 127.0)
    codes = (blocks / scale).astype(np.float32).astype(dtype).astype(np.float64)
    return np.moveaxis((codes * scale).reshape(v.shape), -1, axis)


WIDE = False


def mx_kscale(k):
    if not WIDE:
        return np.ones(k)
    levels = np.array([10, -10, 5, -5, 0])
    if k % 512:
        return np.exp2(np.random.permutation(np.resize(levels, k // 32))).repeat(32)
    a = np.empty((k // 512, 16))
    for p in range(k // 512):
        a[p, :8] = np.random.permutation(np.resize(levels, 8))
        for g in range(8):
            far = levels[np.abs(levels - a[p, g]) >= 10]
            a[p, g + 8] = far[np.random.randint(len(far))]
    return np.exp2(a.ravel()).repeat(32)


def f64(x):
    return np.asarray(x).astype(np.float64)


def striped(idx):
    return np.tile(idx.reshape(-1, 16).T, (8, 1)).astype(np.uint16)


def unstriped(offs):
    return offs[:16].T.reshape(-1).astype(np.int64)


E2M1 = np.array([0.0, 0.5, 1.0, 1.5, 2.0, 3.0, 4.0, 6.0, -0.0, -0.5, -1.0, -1.5, -2.0, -3.0, -4.0, -6.0])


def pack_weight(w, fmt):
    k, n = w.shape
    w = f64(np.asarray(w, np.float32).astype(ml_dtypes.bfloat16)).reshape(k // 32, 32, n)
    amax = np.abs(w).max(1)
    if fmt == "e4m3":
        byte = np.frexp(amax)[1] - 1 + 127 - 7
    else:
        mant, ex = np.frexp(amax / 6.0)
        byte = np.where(mant > 0.5, ex, ex - 1) + 127
    byte = np.clip(np.where(amax > 0, byte, 1), 1, 254)
    scaled = (w * np.exp2(127.0 - byte)[:, None, :]).reshape(k, n).astype(np.float32)
    by_word = np.ascontiguousarray(scaled.reshape(k // 512, 128, 4, n).transpose(0, 1, 3, 2))
    if fmt == "e4m3":
        words = by_word.astype(ml_dtypes.float8_e4m3fn).view(np.uint8)
    else:
        c = by_word.astype(ml_dtypes.float4_e2m1fn).view(np.uint8) & 0xF
        words = (c[..., 0::2] | (c[..., 1::2] << 4)).reshape(k // 512, 128, 2 * n)
    return np.ascontiguousarray(words), np.ascontiguousarray(byte.astype(np.uint8).reshape(k // 512, 16, n))


def unpack_weight(words, scales, fmt):
    g, _, n = scales.shape
    words = np.ascontiguousarray(words).reshape(g, 128, n, -1)
    if fmt == "e4m3":
        vals = words.view(ml_dtypes.float8_e4m3fn).astype(np.float64)
    else:
        nib = np.empty((g, 128, n, 4), np.uint8)
        nib[..., 0::2] = words & 0xF
        nib[..., 1::2] = words >> 4
        vals = E2M1[nib]
    vals = vals * np.repeat(np.exp2(scales.astype(np.float64) - 127.0), 8, axis=1)[..., None]
    return vals.transpose(0, 1, 3, 2).reshape(g * 512, n)


def gelu(v):
    return 0.5 * v * (1.0 + np.tanh(np.sqrt(2.0 / np.pi) * (v + 0.044715 * v**3)))


K, T, E, C, H, N = 512, 1024, 8, 128, 512, 128
TOP = 4
PAD = 64


def by_expert(wq, xq):
    return np.concatenate([wq[e].T @ xq[:, e * C:(e + 1) * C] for e in range(E)], axis=1)


def setup_inputs():
    n = np.random.standard_normal
    s = mx_kscale(K)[:, None]
    u = mx_kscale(H)
    slot_token = np.empty(E * C, np.int64); pos = np.tile(E * C + np.arange(T) % PAD, (TOP, 1)); taken = np.zeros(T, np.int64)
    liked = np.random.randn(T)
    for e in np.random.permutation(E):
        free = np.flatnonzero(taken < TOP); pick = np.random.permutation(free[np.argsort(-(liked[free] + np.random.gumbel(size=free.size)))[:C]]); slot_token[e * C:(e + 1) * C] = pick
        pos[taken[pick], pick] = e * C + np.arange(C); taken[pick] += 1
    g = np.random.uniform(0.2, 0.8, (TOP, T))
    x = pack_weight(n((K, T)) * s, "e4m3")
    return {
        "x_words": x[0],
        "x_scales": x[1],
        "w1": (n((E, K, H)) / np.sqrt(K) / s[None] * u[None, None, :]).astype(np.float32),
        "w2": (n((E, H, N)) / np.sqrt(H) / u[None, :, None]).astype(np.float32),
        "gate": np.stack([np.tile(r, (N, 1)) for r in g]).astype(np.float32),
        "offs": striped(slot_token),
        "pos1": striped(pos[0]),
        "pos2": striped(pos[1]),
        "pos3": striped(pos[2]),
        "pos4": striped(pos[3]),
    }


def reference(x_words, x_scales, w1, w2, gate, offs, pos1, pos2, pos3, pos4):
    idx = unstriped(offs)
    xq = unpack_weight(x_words, x_scales, "e4m3")[:, idx]
    h = gelu(by_expert(mxq(f64(w1), 1, "e4m3"), xq))
    y = by_expert(mxq(f64(w2), 1, "e4m3"), mxq(h, 0, "e4m3"))
    y = np.concatenate([y, np.zeros((N, PAD))], axis=1)
    return sum(f64(gate[r]) * y[:, unstriped(p)] for r, p in enumerate((pos1, pos2, pos3, pos4)))

@@ -1,0 +1,214 @@
+from contextlib import ExitStack
+
+import concourse.mybir as mybir
+from concourse.masks import make_identity
+
+K, T, E, C, H, N = 512, 1024, 8, 128, 512, 128
+TOP, PAD = 4, 64
+S = E * C
+FLOPS = 2 * S * (K * H + H * N)
+
+F32 = mybir.dt.float32
+BF16 = mybir.dt.bfloat16
+I32 = mybir.dt.int32
+U32 = mybir.dt.uint32
+U16 = mybir.dt.uint16
+U8 = mybir.dt.uint8
+FP8X4 = mybir.dt.float8_e4m3fn_x4
+GELU = mybir.ActivationFunctionType.Gelu_apprx_tanh
+COPY = mybir.ActivationFunctionType.Copy
+
+P = 128
+PACK = 4
+LIST = 16
+XCH = 512
+TCH = 256
+W2_GROUPS = ((0, 1), (2, 3), (4, 5), (6,), (7,))
+W2_ON_SCALAR = (2,)
+
+
+def tile_moe_ecr_mlp_gelu_kernel(
+    tc, x_words, x_scales, w1, w2, gate, offs, pos1, pos2, pos3, pos4, out
+):
+    nc = tc.nc
+    with ExitStack() as ctx:
+        keep = ctx.enter_context(tc.tile_pool(name="keep", bufs=1))
+        ring = ctx.enter_context(tc.tile_pool(name="ring", bufs=3))
+        psum = ctx.enter_context(tc.psum_pool(name="psum", bufs=1))
+
+        slot_list = keep.tile([P, S // LIST], U16, name="slot_list")
+        pos_lists = [keep.tile([P, T // LIST], U16, name=f"pos_list{r}") for r in range(TOP)]
+        tok_words = keep.tile([P, T], I32, name="tok_words", align_bytes=64)
+        tok_scales = keep.tile([P, T], U8, name="tok_scales", align_bytes=64)
+        y_all = keep.tile([P, S + PAD], F32, name="y_all", align_bytes=64)
+        gate_rows = keep.tile([P, P], F32, name="gate_rows")
+        gate_cols = keep.tile([P, TOP * T // P], F32, name="gate_cols")
+        ident = keep.tile([P, P], F32, name="ident")
+        warm = keep.tile([P, 1], F32, name="warm")
+        w1_raw = [keep.tile([P, PACK, H], F32, name=f"w1_raw{e}", align_bytes=64) for e in range(E)]
+        w2_raw = [keep.tile([P, len(g), PACK, N], F32, name=f"w2_raw{g[0]}", align_bytes=64) for g in W2_GROUPS]
+        gate_last = keep.tile([P, TCH], F32, name="gate_last", align_bytes=64)
+
+        nc.gpsimd.memset(tok_scales[:].bitcast(I32), 0)
+        nc.vector.memset(warm[:], 0.0)
+        nc.scalar.activation(warm[:], warm[:], GELU)
+        nc.vector.memset(y_all[:, S:], 0.0)
+        nc.vector.memset(gate_rows[:], 0.0)
+        make_identity(nc, ident[:])
+
+        def load_w1(e):
+            nc.sync.dma_start(out=w1_raw[e][:], in_=w1[e].rearrange("(p j) c -> p j c", j=PACK))
+
+        def load_w2(i):
+            g = W2_GROUPS[i]
+            nc.sync.dma_start(
+                out=w2_raw[i][:].rearrange("p e j c -> p e (j c)"),
+                in_=w2[g[0]:g[-1] + 1].rearrange("e (p j) c -> p e (j c)", j=PACK),
+            )
+
+        nc.sync.dma_start(out=tok_words[:], in_=x_words[0].rearrange("p t r -> p (t r)").bitcast(I32))
+        nc.sync.dma_start(slot_list[:], offs)
+        scale_rows = x_scales[0].bitcast(I32)
+        for r in range(4):
+            nc.sync.dma_start(out=tok_scales[:].bitcast(I32)[r:P:32, :], in_=scale_rows[r:16:4, :])
+        for e in range(E):
+            load_w1(e)
+            if e == 3:
+                for r, pos in enumerate((pos1, pos2, pos3, pos4)):
+                    nc.sync.dma_start(pos_lists[r][:], pos)
+            if e == 5:
+                for r in range(TOP):
+                    nc.sync.dma_start(
+                        out=gate_rows[r * (T // P):(r + 1) * (T // P), :],
+                        in_=gate[r, 0, :].rearrange("(b t) -> b t", t=P),
+                    )
+        for i in range(len(W2_GROUPS)):
+            load_w2(i)
+        nc.sync.dma_start(out=gate_last[:], in_=gate[TOP - 1, :, T - TCH:])
+
+        slot_words, slot_scales = [], []
+
+        def gather_tokens(g):
+            cols = slot_list[:, g * XCH // LIST:(g + 1) * XCH // LIST]
+            words = keep.tile([P, XCH], U32, name=f"slot_words{g}", align_bytes=64)
+            scales = keep.tile([P, XCH], U8, name=f"slot_scales{g}", align_bytes=64)
+            nc.vector.tensor_copy(words[:], tok_words[:].bitcast(U32).indirect(cols))
+            nc.vector.tensor_copy(scales[:], tok_scales[:].indirect(cols))
+            slot_words.append(words)
+            slot_scales.append(scales)
+
+        def quantize(grouped, width, name):
+            codes = ring.tile([P, width], U32, name=name + "_codes", align_bytes=64)
+            scales = ring.tile([P, width], U8, name=name + "_scales", align_bytes=64)
+            nc.vector.quantize_mx(out=codes[:].bitcast(FP8X4), scales=scales[:], in_=grouped[:])
+            return codes, scales
+
+        h_q = {}
+
+        pre = {}
+
+        def layer1(e):
+            src = w1_raw[e][:].rearrange("p j (m t) -> p m j t", t=PACK)
+            halves = []
+            for u in range(2):
+                if u == 0:
+                    grouped = ring.tile([P, 2 * P * PACK], BF16, name=f"paced{e % 2}", align_bytes=64, bufs=1)
+                else:
+                    grouped = ring.tile([P, 2 * P * PACK], BF16, name="w1_grouped", align_bytes=64)
+                dst = grouped[:].rearrange("p (t m j) -> p m j t", t=2, j=PACK)
+                if u == 0 and e > 0:
+                    nc.vector.tensor_copy(dst, src[:, :, :, 0:2])
+                else:
+                    nc.scalar.copy(dst, src[:, :, :, 2 * u:2 * u + 2])
+                halves.append(quantize(grouped, 2 * P, f"w1q{u}"))
+            acc = psum.tile([P, PACK, C], F32, name="wide", bufs=4)
+            g, lo = divmod(e * C, XCH)
+            for t in range(PACK):
+                codes, scales = halves[t // 2]
+                cols = slice((t % 2) * P, (t % 2 + 1) * P)
+                nc.tensor.matmul_mx(
+                    out=acc[:, t, :], lhsT=codes[:, cols].bitcast(FP8X4), lhsT_scale=scales[:, cols],
+                    rhs=slot_words[g][:, lo:lo + C].bitcast(FP8X4), rhs_scale=slot_scales[g][:, lo:lo + C],
+                    start=True, stop=True,
+                )
+            pre[e] = acc
+
+        def hidden(e):
+            acc = pre[e]
+            h = ring.tile([P, C * PACK], BF16, name=f"paced{(e + 1) % 2}", align_bytes=64, bufs=1)
+            nc.scalar.activation(h[:].rearrange("p (s t) -> p s t", t=PACK), acc[:].rearrange("p t s -> p s t"), GELU)
+            codes = keep.tile([P, C], U32, name=f"h_codes{e}", align_bytes=64)
+            scales = keep.tile([P, C], U8, name=f"h_scales{e}", align_bytes=64)
+            nc.vector.quantize_mx(out=codes[:].bitcast(FP8X4), scales=scales[:], in_=h[:])
+            h_q[e] = (codes, scales)
+
+        def layer2(i):
+            g = W2_GROUPS[i]
+            grouped = ring.tile([P, len(g) * N * PACK], BF16, name="w2_grouped", align_bytes=64)
+            src = w2_raw[i][:].rearrange("p e j (c i) -> p e c j i", i=4)
+            dst = grouped[:].rearrange("p (e c i j) -> p e c j i", e=len(g), i=4, j=PACK)
+            if i in W2_ON_SCALAR:
+                nc.scalar.copy(dst, src)
+            else:
+                nc.vector.tensor_copy(dst, src)
+            codes, scales = quantize(grouped, len(g) * N, "w2q")
+            acc = psum.tile([P, 512], F32, name="narrow", bufs=3)
+            for k, e in enumerate(g):
+                cols = slice(k * N, (k + 1) * N)
+                nc.tensor.matmul_mx(
+                    out=acc[:, k * C:(k + 1) * C], lhsT=codes[:, cols].bitcast(FP8X4), lhsT_scale=scales[:, cols],
+                    rhs=h_q[e][0][:].bitcast(FP8X4), rhs_scale=h_q[e][1][:], start=True, stop=True,
+                )
+            nc.scalar.copy(y_all[:, g[0] * C:(g[-1] + 1) * C], acc[:, :len(g) * C])
+
+        for e in range(E):
+            if (e * C) % XCH == 0:
+                gather_tokens(e * C // XCH)
+            layer1(e)
+            if e > 0:
+                hidden(e - 1)
+            if e == 6:
+                turned = psum.tile([P, 512], F32, name="narrow", bufs=3)
+                nc.tensor.transpose(turned[:, :P], gate_rows[:], ident[:])
+                nc.scalar.copy(gate_cols[:], turned[:, :TOP * T // P])
+        hidden(E - 1)
+        for i in range(len(W2_GROUPS)):
+            layer2(i)
+
+        nblk = TCH // P
+        nch = T // TCH
+        for c in range(nch):
+            last = c == nch - 1
+            turns = TOP - 1 if last else TOP
+            tok = slice(c * TCH // LIST, (c + 1) * TCH // LIST)
+            sums = [psum.tile([P, PACK, C], F32, name="wide", bufs=4) for b in range(nblk)]
+            for r in range(turns):
+                picked = ring.tile([P, TCH], F32, name="picked", bufs=4)
+                nc.vector.tensor_copy(picked[:], y_all[:].indirect(pos_lists[r][:, tok]))
+                turned = psum.tile([P, 512], F32, name="narrow", bufs=3)
+                for b in range(nblk):
+                    nc.tensor.transpose(turned[:, b * P:(b + 1) * P], picked[:, b * P:(b + 1) * P], ident[:])
+                gated = ring.tile([P, TCH], F32, name="gated", bufs=4)
+                for b in range(nblk):
+                    col = r * (T // P) + c * nblk + b
+                    nc.scalar.activation(
+                        gated[:, b * P:(b + 1) * P], turned[:, b * P:(b + 1) * P], COPY, scale=gate_cols[:, col:col + 1]
+                    )
+                for b in range(nblk):
+                    nc.tensor.matmul(
+                        sums[b][:, 0, :], gated[:, b * P:(b + 1) * P], ident[:],
+                        start=(r == 0), stop=(r == turns - 1), is_transpose=True,
+                    )
+            result = ring.tile([P, TCH], F32, name="result", bufs=4)
+            if last:
+                product = ring.tile([P, TCH], F32, name="picked", bufs=4)
+                nc.vector.tensor_tensor(
+                    product[:], y_all[:].indirect(pos_lists[TOP - 1][:, tok]), gate_last[:], mybir.AluOpType.mult
+                )
+            for b in range(nblk):
+                cols = slice(b * P, (b + 1) * P)
+                if last:
+                    nc.vector.tensor_tensor(result[:, cols], sums[b][:, 0, :], product[:, cols], mybir.AluOpType.add)
+                else:
+                    nc.scalar.copy(result[:, cols], sums[b][:, 0, :])
+            nc.sync.dma_start(out=out[:, c * TCH:(c + 1) * TCH], in_=result[:])

@@ -23,8 +23,13 @@ PACK = 4
 LIST = 16
 XCH = 512
 TCH = 256
-W2_GROUPS = ((0, 1), (2, 3), (4, 5), (6,), (7,))
-W2_ON_SCALAR = (2,)
+W2_GROUPS = ((0, 1), (2,), (3,), (4,), (5,), (6,), (7,))
+Y_GROUPS = ((0, 1), (2,), (3, 4, 5), (6, 7))
+CHUNKS = (384, 384, 128, 128)
+SPLIT_W1 = (7,)
+W2_ON_SCALAR = (2, 5)
+W2_EARLY = {0: 2, 1: 4}
+BOTH_ON_VECTOR = ()
 
 
 def tile_moe_ecr_mlp_gelu_kernel(
@@ -41,23 +46,30 @@ def tile_moe_ecr_mlp_gelu_kernel(
         tok_words = keep.tile([P, T], I32, name="tok_words", align_bytes=64)
         tok_scales = keep.tile([P, T], U8, name="tok_scales", align_bytes=64)
         y_all = keep.tile([P, S + PAD], F32, name="y_all", align_bytes=64)
-        gate_rows = keep.tile([P, P], F32, name="gate_rows")
-        gate_cols = keep.tile([P, TOP * T // P], F32, name="gate_cols")
         ident = keep.tile([P, P], F32, name="ident")
         warm = keep.tile([P, 1], F32, name="warm")
-        w1_raw = [keep.tile([P, PACK, H], F32, name=f"w1_raw{e}", align_bytes=64) for e in range(E)]
+        w1_raw = []
+        for e in range(E):
+            parts = 2 if e in SPLIT_W1 else 1
+            w1_raw.append([
+                keep.tile([P, PACK, H // parts], F32, name=f"w1_raw{e}_{i}", tag=f"w1_raw{e}_{parts - 1 - i}", align_bytes=64)
+                for i in range(parts)
+            ])
         w2_raw = [keep.tile([P, len(g), PACK, N], F32, name=f"w2_raw{g[0]}", align_bytes=64) for g in W2_GROUPS]
-        gate_last = keep.tile([P, TCH], F32, name="gate_last", align_bytes=64)
+        gates = [[keep.tile([P, 2, w], F32, name=f"gate{c}_{u}", align_bytes=64) for u in range(2)] for c, w in enumerate(CHUNKS)]
+        starts = [sum(CHUNKS[:c]) for c in range(len(CHUNKS))]
 
         nc.gpsimd.memset(tok_scales[:].bitcast(I32), 0)
         nc.vector.memset(warm[:], 0.0)
         nc.scalar.activation(warm[:], warm[:], GELU)
         nc.vector.memset(y_all[:, S:], 0.0)
-        nc.vector.memset(gate_rows[:], 0.0)
         make_identity(nc, ident[:])
 
         def load_w1(e):
-            nc.sync.dma_start(out=w1_raw[e][:], in_=w1[e].rearrange("(p j) c -> p j c", j=PACK))
+            rows = w1[e].rearrange("(p j) c -> p j c", j=PACK)
+            width = H // len(w1_raw[e])
+            for i, raw in enumerate(w1_raw[e]):
+                nc.sync.dma_start(out=raw[:], in_=rows[:, :, i * width:(i + 1) * width])
 
         def load_w2(i):
             g = W2_GROUPS[i]
@@ -73,18 +85,19 @@ def tile_moe_ecr_mlp_gelu_kernel(
             nc.sync.dma_start(out=tok_scales[:].bitcast(I32)[r:P:32, :], in_=scale_rows[r:16:4, :])
         for e in range(E):
             load_w1(e)
-            if e == 3:
-                for r, pos in enumerate((pos1, pos2, pos3, pos4)):
-                    nc.sync.dma_start(pos_lists[r][:], pos)
-            if e == 5:
-                for r in range(TOP):
-                    nc.sync.dma_start(
-                        out=gate_rows[r * (T // P):(r + 1) * (T // P), :],
-                        in_=gate[r, 0, :].rearrange("(b t) -> b t", t=P),
-                    )
+            for i in range(len(W2_GROUPS)):
+                if W2_EARLY.get(i) == e:
+                    load_w2(i)
         for i in range(len(W2_GROUPS)):
-            load_w2(i)
-        nc.sync.dma_start(out=gate_last[:], in_=gate[TOP - 1, :, T - TCH:])
+            if i not in W2_EARLY:
+                load_w2(i)
+        for r, pos in enumerate((pos1, pos2, pos3, pos4)):
+            nc.sync.dma_start(pos_lists[r][:], pos)
+        for c, w in enumerate(CHUNKS):
+            for u in range(2):
+                nc.sync.dma_start(
+                    out=gates[c][u][:], in_=gate[2 * u:2 * u + 2, :, starts[c]:starts[c] + w].rearrange("r n t -> n r t")
+                )
 
         slot_words, slot_scales = [], []
 
@@ -106,20 +119,25 @@ def tile_moe_ecr_mlp_gelu_kernel(
         h_q = {}
 
         pre = {}
+        hs = {}
+        y_acc = {}
+        probe_src = []
 
         def layer1(e):
-            src = w1_raw[e][:].rearrange("p j (m t) -> p m j t", t=PACK)
             halves = []
             for u in range(2):
                 if u == 0:
-                    grouped = ring.tile([P, 2 * P * PACK], BF16, name=f"paced{e % 2}", align_bytes=64, bufs=1)
+                    grouped = keep.tile([P, 2 * P * PACK], BF16, name=f"w1_first{e}", tag=f"w1_first{e}", align_bytes=64)
                 else:
                     grouped = ring.tile([P, 2 * P * PACK], BF16, name="w1_grouped", align_bytes=64)
                 dst = grouped[:].rearrange("p (t m j) -> p m j t", t=2, j=PACK)
-                if u == 0 and e > 0:
-                    nc.vector.tensor_copy(dst, src[:, :, :, 0:2])
-                else:
-                    nc.scalar.copy(dst, src[:, :, :, 2 * u:2 * u + 2])
+                rows = P // len(w1_raw[e])
+                for i, raw in enumerate(w1_raw[e]):
+                    src = raw[:].rearrange("p j (m t) -> p m j t", t=PACK)[:, :, :, 2 * u:2 * u + 2]
+                    if (u == 0 and e > 0) or e in BOTH_ON_VECTOR:
+                        nc.vector.tensor_copy(dst[:, i * rows:(i + 1) * rows], src)
+                    else:
+                        nc.scalar.copy(dst[:, i * rows:(i + 1) * rows], src)
                 halves.append(quantize(grouped, 2 * P, f"w1q{u}"))
             acc = psum.tile([P, PACK, C], F32, name="wide", bufs=4)
             g, lo = divmod(e * C, XCH)
@@ -135,9 +153,13 @@ def tile_moe_ecr_mlp_gelu_kernel(
 
         def hidden(e):
             acc = pre[e]
-            h = ring.tile([P, C * PACK], BF16, name=f"paced{(e + 1) % 2}", align_bytes=64, bufs=1)
+            h = keep.tile([P, C * PACK], BF16, name=f"h{e}", tag=f"w1_raw{e + 1}_0", align_bytes=64)
+            hs[e] = h
             nc.scalar.activation(h[:].rearrange("p (s t) -> p s t", t=PACK), acc[:].rearrange("p t s -> p s t"), GELU)
-            codes = keep.tile([P, C], U32, name=f"h_codes{e}", align_bytes=64)
+
+        def hidden_q(e):
+            h = hs[e]
+            codes = keep.tile([P, C], U32, name=f"h_codes{e}", tag=f"w1_first{e + 2}" if e < 5 else f"h_codes{e}", align_bytes=64)
             scales = keep.tile([P, C], U8, name=f"h_scales{e}", align_bytes=64)
             nc.vector.quantize_mx(out=codes[:].bitcast(FP8X4), scales=scales[:], in_=h[:])
             h_q[e] = (codes, scales)
@@ -152,14 +174,19 @@ def tile_moe_ecr_mlp_gelu_kernel(
             else:
                 nc.vector.tensor_copy(dst, src)
             codes, scales = quantize(grouped, len(g) * N, "w2q")
-            acc = psum.tile([P, 512], F32, name="narrow", bufs=3)
             for k, e in enumerate(g):
+                together = [grp for grp in Y_GROUPS if e in grp][0]
+                if e == together[0]:
+                    y_acc[together] = psum.tile([P, 512], F32, name="narrow", bufs=3)
+                acc = y_acc[together]
+                at = (e - together[0]) * C
                 cols = slice(k * N, (k + 1) * N)
                 nc.tensor.matmul_mx(
-                    out=acc[:, k * C:(k + 1) * C], lhsT=codes[:, cols].bitcast(FP8X4), lhsT_scale=scales[:, cols],
+                    out=acc[:, at:at + C], lhsT=codes[:, cols].bitcast(FP8X4), lhsT_scale=scales[:, cols],
                     rhs=h_q[e][0][:].bitcast(FP8X4), rhs_scale=h_q[e][1][:], start=True, stop=True,
                 )
-            nc.scalar.copy(y_all[:, g[0] * C:(g[-1] + 1) * C], acc[:, :len(g) * C])
+                if e == together[-1]:
+                    nc.scalar.copy(y_all[:, together[0] * C:(e + 1) * C], acc[:, :at + C])
 
         for e in range(E):
             if (e * C) % XCH == 0:
@@ -167,48 +194,53 @@ def tile_moe_ecr_mlp_gelu_kernel(
             layer1(e)
             if e > 0:
                 hidden(e - 1)
-            if e == 6:
-                turned = psum.tile([P, 512], F32, name="narrow", bufs=3)
-                nc.tensor.transpose(turned[:, :P], gate_rows[:], ident[:])
-                nc.scalar.copy(gate_cols[:], turned[:, :TOP * T // P])
+            if 1 < e < E - 1:
+                hidden_q(e - 2)
+            if e == E - 2:
+                hidden_q(e - 1)
+            for i in range(len(W2_GROUPS)):
+                if W2_EARLY.get(i) == e - 1:
+                    layer2(i)
         hidden(E - 1)
+        hidden_q(E - 2)
+        hidden_q(E - 1)
         for i in range(len(W2_GROUPS)):
-            layer2(i)
+            if i not in W2_EARLY:
+                layer2(i)
 
-        nblk = TCH // P
-        nch = T // TCH
-        for c in range(nch):
-            last = c == nch - 1
-            turns = TOP - 1 if last else TOP
-            tok = slice(c * TCH // LIST, (c + 1) * TCH // LIST)
-            sums = [psum.tile([P, PACK, C], F32, name="wide", bufs=4) for b in range(nblk)]
-            for r in range(turns):
-                picked = ring.tile([P, TCH], F32, name="picked", bufs=4)
-                nc.vector.tensor_copy(picked[:], y_all[:].indirect(pos_lists[r][:, tok]))
-                turned = psum.tile([P, 512], F32, name="narrow", bufs=3)
-                for b in range(nblk):
-                    nc.tensor.transpose(turned[:, b * P:(b + 1) * P], picked[:, b * P:(b + 1) * P], ident[:])
-                gated = ring.tile([P, TCH], F32, name="gated", bufs=4)
-                for b in range(nblk):
-                    col = r * (T // P) + c * nblk + b
-                    nc.scalar.activation(
-                        gated[:, b * P:(b + 1) * P], turned[:, b * P:(b + 1) * P], COPY, scale=gate_cols[:, col:col + 1]
-                    )
-                for b in range(nblk):
-                    nc.tensor.matmul(
-                        sums[b][:, 0, :], gated[:, b * P:(b + 1) * P], ident[:],
-                        start=(r == 0), stop=(r == turns - 1), is_transpose=True,
-                    )
-            result = ring.tile([P, TCH], F32, name="result", bufs=4)
-            if last:
-                product = ring.tile([P, TCH], F32, name="picked", bufs=4)
+        add = mybir.AluOpType.add
+        for c, w in enumerate(CHUNKS):
+            last = c == len(CHUNKS) - 1
+            nblk = w // P
+            tok = slice(starts[c] // LIST, (starts[c] + w) // LIST)
+            terms = []
+            if not last:
+                sums = [psum.tile([P, PACK, C], F32, name="wide", bufs=4) for b in range(nblk)]
+            for r in range(TOP):
+                term = ring.tile([P, w], F32, name="picked", bufs=8)
                 nc.vector.tensor_tensor(
-                    product[:], y_all[:].indirect(pos_lists[TOP - 1][:, tok]), gate_last[:], mybir.AluOpType.mult
+                    term[:], y_all[:].indirect(pos_lists[r][:, tok]), gates[c][r // 2][:, r % 2, :], mybir.AluOpType.mult
                 )
-            for b in range(nblk):
-                cols = slice(b * P, (b + 1) * P)
-                if last:
-                    nc.vector.tensor_tensor(result[:, cols], sums[b][:, 0, :], product[:, cols], mybir.AluOpType.add)
-                else:
-                    nc.scalar.copy(result[:, cols], sums[b][:, 0, :])
-            nc.sync.dma_start(out=out[:, c * TCH:(c + 1) * TCH], in_=result[:])
+                terms.append(term)
+                if not last:
+                    for b in range(nblk):
+                        nc.tensor.matmul(
+                            sums[b][:, 0, :], term[:, b * P:(b + 1) * P], ident[:],
+                            start=(r == 0), stop=(r == TOP - 1), is_transpose=True,
+                        )
+            result = ring.tile([P, w], F32, name="result", bufs=4)
+            if last:
+                total = terms[0]
+                for r in range(1, TOP):
+                    into = result if r == TOP - 1 else ring.tile([P, w], F32, name="partial")
+                    nc.vector.tensor_tensor(into[:], total[:], terms[r][:], add)
+                    total = into
+            else:
+                summed = ring.tile([P, w], F32, name="summed")
+                back = psum.tile([P, 512], F32, name="narrow", bufs=3)
+                for b in range(nblk):
+                    cols = slice(b * P, (b + 1) * P)
+                    nc.scalar.copy(summed[:, cols], sums[b][:, 0, :])
+                    nc.tensor.transpose(back[:, cols], summed[:, cols], ident[:])
+                nc.scalar.copy(result[:], back[:, :w])
+            nc.sync.dma_start(out=out[:, starts[c]:starts[c] + w], in_=result[:])

@@ -27,7 +27,7 @@ W2_GROUPS = ((0, 1), (2,), (3,), (4,), (5,), (6,), (7,))
 Y_GROUPS = ((0, 1), (2,), (3, 4, 5), (6, 7))
 CHUNKS = (384, 384, 128, 128)
 SPLIT_W1 = (7,)
-W2_ON_SCALAR = (2, 5)
+W2_ON_SCALAR = (0, 2, 5)
 W2_EARLY = {0: 2, 1: 4}
 BOTH_ON_VECTOR = ()
 

from contextlib import ExitStack

import concourse.mybir as mybir
from concourse.masks import make_identity

K, T, E, C, H, N = 512, 1024, 8, 128, 512, 128
TOP, PAD = 4, 64
S = E * C
FLOPS = 2 * S * (K * H + H * N)

F32 = mybir.dt.float32
BF16 = mybir.dt.bfloat16
I32 = mybir.dt.int32
U32 = mybir.dt.uint32
U16 = mybir.dt.uint16
U8 = mybir.dt.uint8
FP8X4 = mybir.dt.float8_e4m3fn_x4
GELU = mybir.ActivationFunctionType.Gelu_apprx_tanh
COPY = mybir.ActivationFunctionType.Copy

P = 128
PACK = 4
LIST = 16
XCH = 512
TCH = 256
W2_GROUPS = ((0, 1), (2,), (3,), (4,), (5,), (6,), (7,))
Y_GROUPS = ((0, 1), (2,), (3, 4, 5), (6, 7))
CHUNKS = (384, 384, 128, 128)
SPLIT_W1 = (7,)
W2_ON_SCALAR = (0, 2, 5)
W2_EARLY = {0: 2, 1: 4}
BOTH_ON_VECTOR = ()


def tile_moe_ecr_mlp_gelu_kernel(
    tc, x_words, x_scales, w1, w2, gate, offs, pos1, pos2, pos3, pos4, out
):
    nc = tc.nc
    with ExitStack() as ctx:
        keep = ctx.enter_context(tc.tile_pool(name="keep", bufs=1))
        ring = ctx.enter_context(tc.tile_pool(name="ring", bufs=3))
        psum = ctx.enter_context(tc.psum_pool(name="psum", bufs=1))

        slot_list = keep.tile([P, S // LIST], U16, name="slot_list")
        pos_lists = [keep.tile([P, T // LIST], U16, name=f"pos_list{r}") for r in range(TOP)]
        tok_words = keep.tile([P, T], I32, name="tok_words", align_bytes=64)
        tok_scales = keep.tile([P, T], U8, name="tok_scales", align_bytes=64)
        y_all = keep.tile([P, S + PAD], F32, name="y_all", align_bytes=64)
        ident = keep.tile([P, P], F32, name="ident")
        warm = keep.tile([P, 1], F32, name="warm")
        w1_raw = []
        for e in range(E):
            parts = 2 if e in SPLIT_W1 else 1
            w1_raw.append([
                keep.tile([P, PACK, H // parts], F32, name=f"w1_raw{e}_{i}", tag=f"w1_raw{e}_{parts - 1 - i}", align_bytes=64)
                for i in range(parts)
            ])
        w2_raw = [keep.tile([P, len(g), PACK, N], F32, name=f"w2_raw{g[0]}", align_bytes=64) for g in W2_GROUPS]
        gates = [[keep.tile([P, 2, w], F32, name=f"gate{c}_{u}", align_bytes=64) for u in range(2)] for c, w in enumerate(CHUNKS)]
        starts = [sum(CHUNKS[:c]) for c in range(len(CHUNKS))]

        nc.gpsimd.memset(tok_scales[:].bitcast(I32), 0)
        nc.vector.memset(warm[:], 0.0)
        nc.scalar.activation(warm[:], warm[:], GELU)
        nc.vector.memset(y_all[:, S:], 0.0)
        make_identity(nc, ident[:])

        def load_w1(e):
            rows = w1[e].rearrange("(p j) c -> p j c", j=PACK)
            width = H // len(w1_raw[e])
            for i, raw in enumerate(w1_raw[e]):
                nc.sync.dma_start(out=raw[:], in_=rows[:, :, i * width:(i + 1) * width])

        def load_w2(i):
            g = W2_GROUPS[i]
            nc.sync.dma_start(
                out=w2_raw[i][:].rearrange("p e j c -> p e (j c)"),
                in_=w2[g[0]:g[-1] + 1].rearrange("e (p j) c -> p e (j c)", j=PACK),
            )

        nc.sync.dma_start(out=tok_words[:], in_=x_words[0].rearrange("p t r -> p (t r)").bitcast(I32))
        nc.sync.dma_start(slot_list[:], offs)
        scale_rows = x_scales[0].bitcast(I32)
        for r in range(4):
            nc.sync.dma_start(out=tok_scales[:].bitcast(I32)[r:P:32, :], in_=scale_rows[r:16:4, :])
        for e in range(E):
            load_w1(e)
            for i in range(len(W2_GROUPS)):
                if W2_EARLY.get(i) == e:
                    load_w2(i)
        for i in range(len(W2_GROUPS)):
            if i not in W2_EARLY:
                load_w2(i)
        for r, pos in enumerate((pos1, pos2, pos3, pos4)):
            nc.sync.dma_start(pos_lists[r][:], pos)
        for c, w in enumerate(CHUNKS):
            for u in range(2):
                nc.sync.dma_start(
                    out=gates[c][u][:], in_=gate[2 * u:2 * u + 2, :, starts[c]:starts[c] + w].rearrange("r n t -> n r t")
                )

        slot_words, slot_scales = [], []

        def gather_tokens(g):
            cols = slot_list[:, g * XCH // LIST:(g + 1) * XCH // LIST]
            words = keep.tile([P, XCH], U32, name=f"slot_words{g}", align_bytes=64)
            scales = keep.tile([P, XCH], U8, name=f"slot_scales{g}", align_bytes=64)
            nc.vector.tensor_copy(words[:], tok_words[:].bitcast(U32).indirect(cols))
            nc.vector.tensor_copy(scales[:], tok_scales[:].indirect(cols))
            slot_words.append(words)
            slot_scales.append(scales)

        def quantize(grouped, width, name):
            codes = ring.tile([P, width], U32, name=name + "_codes", align_bytes=64)
            scales = ring.tile([P, width], U8, name=name + "_scales", align_bytes=64)
            nc.vector.quantize_mx(out=codes[:].bitcast(FP8X4), scales=scales[:], in_=grouped[:])
            return codes, scales

        h_q = {}

        pre = {}
        hs = {}
        y_acc = {}
        probe_src = []

        def layer1(e):
            halves = []
            for u in range(2):
                if u == 0:
                    grouped = keep.tile([P, 2 * P * PACK], BF16, name=f"w1_first{e}", tag=f"w1_first{e}", align_bytes=64)
                else:
                    grouped = ring.tile([P, 2 * P * PACK], BF16, name="w1_grouped", align_bytes=64)
                dst = grouped[:].rearrange("p (t m j) -> p m j t", t=2, j=PACK)
                rows = P // len(w1_raw[e])
                for i, raw in enumerate(w1_raw[e]):
                    src = raw[:].rearrange("p j (m t) -> p m j t", t=PACK)[:, :, :, 2 * u:2 * u + 2]
                    if (u == 0 and e > 0) or e in BOTH_ON_VECTOR:
                        nc.vector.tensor_copy(dst[:, i * rows:(i + 1) * rows], src)
                    else:
                        nc.scalar.copy(dst[:, i * rows:(i + 1) * rows], src)
                halves.append(quantize(grouped, 2 * P, f"w1q{u}"))
            acc = psum.tile([P, PACK, C], F32, name="wide", bufs=4)
            g, lo = divmod(e * C, XCH)
            for t in range(PACK):
                codes, scales = halves[t // 2]
                cols = slice((t % 2) * P, (t % 2 + 1) * P)
                nc.tensor.matmul_mx(
                    out=acc[:, t, :], lhsT=codes[:, cols].bitcast(FP8X4), lhsT_scale=scales[:, cols],
                    rhs=slot_words[g][:, lo:lo + C].bitcast(FP8X4), rhs_scale=slot_scales[g][:, lo:lo + C],
                    start=True, stop=True,
                )
            pre[e] = acc

        def hidden(e):
            acc = pre[e]
            h = keep.tile([P, C * PACK], BF16, name=f"h{e}", tag=f"w1_raw{e + 1}_0", align_bytes=64)
            hs[e] = h
            nc.scalar.activation(h[:].rearrange("p (s t) -> p s t", t=PACK), acc[:].rearrange("p t s -> p s t"), GELU)

        def hidden_q(e):
            h = hs[e]
            codes = keep.tile([P, C], U32, name=f"h_codes{e}", tag=f"w1_first{e + 2}" if e < 5 else f"h_codes{e}", align_bytes=64)
            scales = keep.tile([P, C], U8, name=f"h_scales{e}", align_bytes=64)
            nc.vector.quantize_mx(out=codes[:].bitcast(FP8X4), scales=scales[:], in_=h[:])
            h_q[e] = (codes, scales)

        def layer2(i):
            g = W2_GROUPS[i]
            grouped = ring.tile([P, len(g) * N * PACK], BF16, name="w2_grouped", align_bytes=64)
            src = w2_raw[i][:].rearrange("p e j (c i) -> p e c j i", i=4)
            dst = grouped[:].rearrange("p (e c i j) -> p e c j i", e=len(g), i=4, j=PACK)
            if i in W2_ON_SCALAR:
                nc.scalar.copy(dst, src)
            else:
                nc.vector.tensor_copy(dst, src)
            codes, scales = quantize(grouped, len(g) * N, "w2q")
            for k, e in enumerate(g):
                together = [grp for grp in Y_GROUPS if e in grp][0]
                if e == together[0]:
                    y_acc[together] = psum.tile([P, 512], F32, name="narrow", bufs=3)
                acc = y_acc[together]
                at = (e - together[0]) * C
                cols = slice(k * N, (k + 1) * N)
                nc.tensor.matmul_mx(
                    out=acc[:, at:at + C], lhsT=codes[:, cols].bitcast(FP8X4), lhsT_scale=scales[:, cols],
                    rhs=h_q[e][0][:].bitcast(FP8X4), rhs_scale=h_q[e][1][:], start=True, stop=True,
                )
                if e == together[-1]:
                    nc.scalar.copy(y_all[:, together[0] * C:(e + 1) * C], acc[:, :at + C])

        for e in range(E):
            if (e * C) % XCH == 0:
                gather_tokens(e * C // XCH)
            layer1(e)
            if e > 0:
                hidden(e - 1)
            if 1 < e < E - 1:
                hidden_q(e - 2)
            if e == E - 2:
                hidden_q(e - 1)
            for i in range(len(W2_GROUPS)):
                if W2_EARLY.get(i) == e - 1:
                    layer2(i)
        hidden(E - 1)
        hidden_q(E - 2)
        hidden_q(E - 1)
        for i in range(len(W2_GROUPS)):
            if i not in W2_EARLY:
                layer2(i)

        add = mybir.AluOpType.add
        for c, w in enumerate(CHUNKS):
            last = c == len(CHUNKS) - 1
            nblk = w // P
            tok = slice(starts[c] // LIST, (starts[c] + w) // LIST)
            terms = []
            if not last:
                sums = [psum.tile([P, PACK, C], F32, name="wide", bufs=4) for b in range(nblk)]
            for r in range(TOP):
                term = ring.tile([P, w], F32, name="picked", bufs=8)
                nc.vector.tensor_tensor(
                    term[:], y_all[:].indirect(pos_lists[r][:, tok]), gates[c][r // 2][:, r % 2, :], mybir.AluOpType.mult
                )
                terms.append(term)
                if not last:
                    for b in range(nblk):
                        nc.tensor.matmul(
                            sums[b][:, 0, :], term[:, b * P:(b + 1) * P], ident[:],
                            start=(r == 0), stop=(r == TOP - 1), is_transpose=True,
                        )
            result = ring.tile([P, w], F32, name="result", bufs=4)
            if last:
                total = terms[0]
                for r in range(1, TOP):
                    into = result if r == TOP - 1 else ring.tile([P, w], F32, name="partial")
                    nc.vector.tensor_tensor(into[:], total[:], terms[r][:], add)
                    total = into
            else:
                summed = ring.tile([P, w], F32, name="summed")
                back = psum.tile([P, 512], F32, name="narrow", bufs=3)
                for b in range(nblk):
                    cols = slice(b * P, (b + 1) * P)
                    nc.scalar.copy(summed[:, cols], sums[b][:, 0, :])
                    nc.tensor.transpose(back[:, cols], summed[:, cols], ident[:])
                nc.scalar.copy(result[:], back[:, :w])
            nc.sync.dma_start(out=out[:, starts[c]:starts[c] + w], in_=result[:])
